import numpy as np, ml_dtypes
CORES = [3,7,11,15,131,135,139,143]
N = 8
import mx_ref
NC = 256
BF = ml_dtypes.bfloat16
def setup_inputs(rng):
    def f(*shape):
        return mx_ref.flush((rng.standard_normal(shape, dtype=np.float32) * np.exp2(rng.integers(-2, 3, shape[:-1] + (1,)))).astype(BF))
    return {"u": f(N, 128, 512), "v": f(N, 128, 512), "x": f(N, 128, 4 * NC)}
def setup_inputs_blocks(rng):
    d = setup_inputs(rng)
    for k in ("u", "v", "x"): d[k] = mx_ref.spread(d[k], rng, 4)
    return d
def setup_inputs_wide(rng):
    d = setup_inputs(rng)
    for k in ("u", "v", "x"): d[k] = mx_ref.flush((d[k].astype(np.float32) * np.exp2(rng.integers(-8, 9, (N, 1, 1))).astype(np.float32)).astype(BF))
    return d
def setup_inputs_zeros(rng):
    d = setup_inputs(rng); v = d["x"].reshape(N, 128, -1, 4).copy()
    v[np.broadcast_to((rng.random((N, 1, v.shape[2], 1)) < 0.33), v.shape)] = 0
    d["x"] = v.reshape(d["x"].shape)
    return d
def reference(u, v, x):
    QX = [mx_ref.quantize(x[j]) for j in range(N)]
    y = np.zeros((N, 128, N * NC), np.float32)
    for r in range(N):
        qu, qv = mx_ref.quantize(u[r]), mx_ref.quantize(v[r])
        for j in range(N):
            y[r][:, NC * j:NC * j + NC] = np.maximum(mx_ref.matmul(qu, QX[j]), np.float32(0)) * mx_ref.matmul(qv, QX[j])
    return {"y": y}

@@ -1,0 +1,125 @@
+from concourse.bass import DstId, RemoteDMATransfer
+from concourse.mybir import dt, AluOpType, ActivationFunctionType
+
+N = 8
+NC = 256
+
+SCRATCH = {
+    "xb": ("sbuf", [128, 4 * NC], "bfloat16"),
+    "ub": ("sbuf", [128, 512], "bfloat16"),
+    "vb": ("sbuf", [128, 512], "bfloat16"),
+    "qx": ("sbuf", [128, N * NC], "float8_e4m3fn_x4"),
+    "sx": ("sbuf", [128, N * NC], "uint8"),
+    "qu": ("sbuf", [128, 128], "float8_e4m3fn_x4"),
+    "su": ("sbuf", [128, 128], "uint8"),
+    "qv": ("sbuf", [128, 128], "float8_e4m3fn_x4"),
+    "sv": ("sbuf", [128, 128], "uint8"),
+    "yb": ("sbuf", [128, N * NC], "float32"),
+    "ps": ("psum", [128, 8 * 512], "float32"),
+}
+SEMAPHORES = ["lx", "lw", "qx", "qw", "mu", "mv", "rl", "yd", "st", "sent"] + ["a%d" % j for j in range(N)]
+
+
+def _count(mask):
+    return bin(mask).count("1")
+
+
+def _roles(core, T, topo):
+    out = {}
+    for q in T.cores:
+        if q == core:
+            continue
+        if topo.host(q) == topo.host(core) and topo.chip(q) == topo.chip(core):
+            kind = "peer"
+        elif topo.mates(core, q):
+            kind = "mate"
+        elif topo.same_plane(core, q):
+            kind = "plane"
+        else:
+            kind = "far"
+        out[(kind, topo.die(q) == topo.die(core))] = q
+    return out
+
+
+def rank_program(g, core, T, topo):
+    rank = T.rank_of(core)
+    if rank is None:
+        return
+    S = T.sem
+    role = _roles(core, T, topo)
+    peer = role[("peer", False)]
+    far, plane, mate = role[("far", True)], role[("plane", True)], role[("mate", True)]
+    far2, plane2, mate2 = role[("far", False)], role[("plane", False)], role[("mate", False)]
+    off = topo.mask(core, far) & topo.mask(core, plane) & topo.mask(core, mate)
+    stay = topo.mask(core, peer) & ~off
+    sent = [0]
+
+    def cols(j):
+        return slice(j * NC, (j + 1) * NC)
+
+    def send(j, dests, mask, codes):
+        def ap():
+            return T.qx[:, cols(j)].bitcast(dt.uint8) if codes else T.sx[:, cols(j)]
+        ids = []
+        for d in dests:
+            rid, pid = topo.addr(d, core)
+            ids.append(DstId(rid=rid, pnc=pid))
+        tr = RemoteDMATransfer(dst_ids=ids, dma_engine_mask=mask, remote_sem=S["a%d" % j],
+                               srcs=[ap()], dsts=[ap() for _ in dests])
+        g.remote_dma_fused([tr], local_sem=S.sent)
+        sent[0] += _count(mask)
+
+    g.sync.dma_start(T.xb[:], T.x[:]).then_inc(S.lx, 16)
+    g.sync.dma_start(T.ub[:], T.u[:]).then_inc(S.lw, 16)
+    g.sync.dma_start(T.vb[:], T.v[:]).then_inc(S.lw, 16)
+
+    g.vector.wait_ge(S.lx, 16)
+    g.vector.quantize_mx(T.qx[:, cols(rank)], T.sx[:, cols(rank)], T.xb[:]).then_inc(S.qx, 1)
+    g.vector.wait_ge(S.lw, 32)
+    g.vector.quantize_mx(T.qu[:], T.su[:], T.ub[:]).then_inc(S.qw, 1)
+    g.vector.quantize_mx(T.qv[:], T.sv[:], T.vb[:]).then_inc(S.qw, 1)
+
+    g.wait_ge(S.qx, 1)
+    send(rank, [peer], stay, False)
+    send(rank, [far, plane], off, False)
+    send(rank, [far, plane], off, True)
+    send(rank, [peer], stay, True)
+    send(rank, [mate, mate2], off, False)
+    send(rank, [mate, mate2], off, True)
+    full_off, full_stay = 2 * _count(off), 2 * _count(stay)
+    for q in (far, plane):
+        j = T.rank_of(q)
+        g.wait_ge(S["a%d" % j], full_off)
+        send(j, [peer], stay, True)
+        send(j, [peer], stay, False)
+    g.wait_ge(S.sent, sent[0])
+
+    order = [(core, 0), (peer, full_stay), (far, full_off), (plane, full_off), (mate, full_off),
+             (far2, full_stay), (mate2, full_off), (plane2, full_stay)]
+    stores = {1: (core, peer), 3: (plane,), 4: (mate,), 5: (far, far2), 6: (mate2,), 7: (plane2,)}
+    g.tensor.wait_ge(S.qw, 2)
+    g.tensor.wait_ge(S.qx, 1)
+    nst = 0
+    for k, (q, need) in enumerate(order):
+        j = T.rank_of(q)
+        bu = T.ps[:, (2 * (k % 4)) * 512:(2 * (k % 4)) * 512 + NC]
+        bv = T.ps[:, (2 * (k % 4) + 1) * 512:(2 * (k % 4) + 1) * 512 + NC]
+        if need:
+            g.tensor.wait_ge(S["a%d" % j], need)
+        if k >= 4:
+            g.tensor.wait_ge(S.rl, k - 3)
+            g.tensor.wait_ge(S.yd, k - 3)
+        g.tensor.matmul_mx(bu, T.qu[:], T.su[:], T.qx[:, cols(j)], T.sx[:, cols(j)], True, True).then_inc(S.mu, 1)
+        g.tensor.matmul_mx(bv, T.qv[:], T.sv[:], T.qx[:, cols(j)], T.sx[:, cols(j)], True, True).then_inc(S.mv, 1)
+        g.scalar.wait_ge(S.mu, k + 1)
+        g.scalar.activation(T.yb[:, cols(j)], bu, ActivationFunctionType.Relu).then_inc(S.rl, 1)
+        g.vector.wait_ge(S.rl, k + 1)
+        g.vector.wait_ge(S.mv, k + 1)
+        g.vector.tensor_tensor(T.yb[:, cols(j)], T.yb[:, cols(j)], bv, AluOpType.mult).then_inc(S.yd, 1)
+        if k in stores:
+            js = sorted(T.rank_of(c) for c in stores[k])
+            lo, hi = js[0] * NC, (js[-1] + 1) * NC
+            g.sync.wait_ge(S.yd, k + 1)
+            g.sync.dma_start(T.y[:, lo:hi], T.yb[:, lo:hi]).then_inc(S.st, 16)
+            nst += 16
+    g.sync.wait_ge(S.st, nst)

@@ -3,6 +3,8 @@ from concourse.mybir import dt, AluOpType, ActivationFunctionType
 
 N = 8
 NC = 256
+H = NC // 2
+WORLD = 256
 
 SCRATCH = {
     "xb": ("sbuf", [128, 4 * NC], "bfloat16"),
@@ -17,7 +19,8 @@ SCRATCH = {
     "yb": ("sbuf", [128, N * NC], "float32"),
     "ps": ("psum", [128, 8 * 512], "float32"),
 }
-SEMAPHORES = ["lx", "lw", "qx", "qw", "mu", "mv", "rl", "yd", "st", "sent"] + ["a%d" % j for j in range(N)]
+SEMAPHORES = (["lxa", "lxb", "lw", "qa", "qb", "qw", "mu", "mv", "rl", "yd", "st", "st2", "sent", "go1", "go2"]
+              + ["%s%d" % (p, j) for p in "apb" for j in range(N)])
 
 
 def _count(mask):
@@ -41,85 +44,147 @@ def _roles(core, T, topo):
     return out
 
 
+def _relay_of(r, T, topo):
+    role = _roles(r, T, topo)
+    for c in range(WORLD):
+        if (c not in T.cores and topo.host(c) == topo.host(r) and topo.chip(c) == topo.chip(r)
+                and topo.die(c) == topo.die(r) and topo.may_write(c, role[("mate", True)])
+                and topo.may_write(c, role[("mate", False)])):
+            return c
+    return None
+
+
+def _piece(T, j, p):
+    lo = j * NC
+    if p == "a":
+        return T.qx[:, lo:lo + H].bitcast(dt.uint8)
+    if p == "b":
+        return T.qx[:, lo + H:lo + NC].bitcast(dt.uint8)
+    return T.sx[:, lo:lo + NC]
+
+
+def _transfer(T, topo, core, j, p, dests, mask):
+    ids = []
+    for d in dests:
+        rid, pid = topo.addr(d, core)
+        ids.append(DstId(rid=rid, pnc=pid))
+    return RemoteDMATransfer(dst_ids=ids, dma_engine_mask=mask, remote_sem=T.sem["%s%d" % (p, j)],
+                             srcs=[_piece(T, j, p)], dsts=[_piece(T, j, p) for _ in dests])
+
+
+def _relay_program(g, core, r, T, topo):
+    S = T.sem
+    role = _roles(r, T, topo)
+    j = T.rank_of(r)
+    mate, mate2 = role[("mate", True)], role[("mate", False)]
+    out = topo.mask(core, mate) & topo.mask(core, mate2)
+    off_r = topo.mask(r, mate) & topo.mask(r, role[("far", True)]) & topo.mask(r, role[("plane", True)])
+    got = _count(topo.mask(r, core) & ~off_r)
+    for p in "apb":
+        g.wait_ge(S["%s%d" % (p, j)], got)
+        g.remote_dma_fused([_transfer(T, topo, core, j, p, [mate, mate2], out)], local_sem=S.sent)
+    g.wait_ge(S.sent, 3 * _count(out))
+
+
 def rank_program(g, core, T, topo):
     rank = T.rank_of(core)
     if rank is None:
+        for r in T.cores:
+            if _relay_of(r, T, topo) == core:
+                _relay_program(g, core, r, T, topo)
         return
     S = T.sem
     role = _roles(core, T, topo)
     peer = role[("peer", False)]
     far, plane, mate = role[("far", True)], role[("plane", True)], role[("mate", True)]
     far2, plane2, mate2 = role[("far", False)], role[("plane", False)], role[("mate", False)]
+    relay = _relay_of(core, T, topo)
     off = topo.mask(core, far) & topo.mask(core, plane) & topo.mask(core, mate)
-    stay = topo.mask(core, peer) & ~off
+    every = topo.mask(core, peer) & topo.mask(core, relay)
+    stay = every & ~off
+    n_off, n_stay, n_every = _count(off), _count(stay), _count(every)
+    n_relay = _count(topo.mask(relay, mate) & topo.mask(relay, mate2))
     sent = [0]
 
-    def cols(j):
-        return slice(j * NC, (j + 1) * NC)
+    def call(transfers, engines):
+        g.remote_dma_fused(transfers, local_sem=S.sent)
+        sent[0] += engines
 
-    def send(j, dests, mask, codes):
-        def ap():
-            return T.qx[:, cols(j)].bitcast(dt.uint8) if codes else T.sx[:, cols(j)]
-        ids = []
-        for d in dests:
-            rid, pid = topo.addr(d, core)
-            ids.append(DstId(rid=rid, pnc=pid))
-        tr = RemoteDMATransfer(dst_ids=ids, dma_engine_mask=mask, remote_sem=S["a%d" % j],
-                               srcs=[ap()], dsts=[ap() for _ in dests])
-        g.remote_dma_fused([tr], local_sem=S.sent)
-        sent[0] += _count(mask)
+    def tr(j, p, dests, mask):
+        return _transfer(T, topo, core, j, p, dests, mask)
 
-    g.sync.dma_start(T.xb[:], T.x[:]).then_inc(S.lx, 16)
+    g.sync.dma_start(T.xb[:, 0:4 * H], T.x[:, 0:4 * H]).then_inc(S.lxa, 16)
+    g.sync.dma_start(T.xb[:, 4 * H:4 * NC], T.x[:, 4 * H:4 * NC]).then_inc(S.lxb, 16)
     g.sync.dma_start(T.ub[:], T.u[:]).then_inc(S.lw, 16)
     g.sync.dma_start(T.vb[:], T.v[:]).then_inc(S.lw, 16)
 
-    g.vector.wait_ge(S.lx, 16)
-    g.vector.quantize_mx(T.qx[:, cols(rank)], T.sx[:, cols(rank)], T.xb[:]).then_inc(S.qx, 1)
+    lo = rank * NC
+    g.vector.wait_ge(S.lxa, 16)
+    g.vector.quantize_mx(T.qx[:, lo:lo + H], T.sx[:, lo:lo + H], T.xb[:, 0:4 * H]).then_inc(S.qa, 1)
+    g.vector.wait_ge(S.lxb, 16)
+    g.vector.quantize_mx(T.qx[:, lo + H:lo + NC], T.sx[:, lo + H:lo + NC], T.xb[:, 4 * H:4 * NC]).then_inc(S.qb, 1)
     g.vector.wait_ge(S.lw, 32)
     g.vector.quantize_mx(T.qu[:], T.su[:], T.ub[:]).then_inc(S.qw, 1)
     g.vector.quantize_mx(T.qv[:], T.sv[:], T.vb[:]).then_inc(S.qw, 1)
 
-    g.wait_ge(S.qx, 1)
-    send(rank, [peer], stay, False)
-    send(rank, [far, plane], off, False)
-    send(rank, [far, plane], off, True)
-    send(rank, [peer], stay, True)
-    send(rank, [mate, mate2], off, False)
-    send(rank, [mate, mate2], off, True)
-    full_off, full_stay = 2 * _count(off), 2 * _count(stay)
-    for q in (far, plane):
-        j = T.rank_of(q)
-        g.wait_ge(S["a%d" % j], full_off)
-        send(j, [peer], stay, True)
-        send(j, [peer], stay, False)
+    g.wait_ge(S.qa, 1)
+    call([tr(rank, "a", [far, plane], off), tr(rank, "a", [relay, peer], stay)], n_off + n_stay)
+    g.wait_ge(S.qb, 1)
+    call([tr(rank, "p", [far, plane], off), tr(rank, "p", [relay, peer], stay)], n_off + n_stay)
+    call([tr(rank, "b", [far, plane], off), tr(rank, "b", [relay, peer], stay)], n_off + n_stay)
+    g.sem_inc(S.go1, 1)
+    jf, jp = T.rank_of(far), T.rank_of(plane)
+    for p in "ap":
+        g.wait_ge(S["%s%d" % (p, jf)], n_off)
+        g.wait_ge(S["%s%d" % (p, jp)], n_off)
+        call([tr(jf, p, [peer], stay), tr(jp, p, [peer], off)], n_stay + n_off)
+    for j in (jf, jp):
+        g.wait_ge(S["b%d" % j], n_off)
+        call([tr(j, "b", [peer], every)], n_every)
+    g.sem_inc(S.go2, 1)
     g.wait_ge(S.sent, sent[0])
 
-    order = [(core, 0), (peer, full_stay), (far, full_off), (plane, full_off), (mate, full_off),
-             (far2, full_stay), (mate2, full_off), (plane2, full_stay)]
-    stores = {1: (core, peer), 3: (plane,), 4: (mate,), 5: (far, far2), 6: (mate2,), 7: (plane2,)}
+    need = {peer: (n_stay, n_stay, n_stay), far: (n_off, n_off, n_off), plane: (n_off, n_off, n_off),
+            mate: (n_relay, n_relay, n_relay), mate2: (n_relay, n_relay, n_relay),
+            far2: (n_stay, n_stay, n_every), plane2: (n_off, n_off, n_every)}
+
+    units = [(core, 0, NC), (peer, 0, NC), (far, 0, NC), (plane, 0, NC), (far2, 0, H), (plane2, 0, H),
+             (mate, 0, NC), (mate2, 0, NC), (far2, H, NC), (plane2, H, NC)]
     g.tensor.wait_ge(S.qw, 2)
-    g.tensor.wait_ge(S.qx, 1)
+    g.tensor.wait_ge(S.qa, 1)
+    g.tensor.wait_ge(S.qb, 1)
     nst = 0
-    for k, (q, need) in enumerate(order):
+    for m, (q, c0, c1) in enumerate(units):
         j = T.rank_of(q)
-        bu = T.ps[:, (2 * (k % 4)) * 512:(2 * (k % 4)) * 512 + NC]
-        bv = T.ps[:, (2 * (k % 4) + 1) * 512:(2 * (k % 4) + 1) * 512 + NC]
-        if need:
-            g.tensor.wait_ge(S["a%d" % j], need)
-        if k >= 4:
-            g.tensor.wait_ge(S.rl, k - 3)
-            g.tensor.wait_ge(S.yd, k - 3)
-        g.tensor.matmul_mx(bu, T.qu[:], T.su[:], T.qx[:, cols(j)], T.sx[:, cols(j)], True, True).then_inc(S.mu, 1)
-        g.tensor.matmul_mx(bv, T.qv[:], T.sv[:], T.qx[:, cols(j)], T.sx[:, cols(j)], True, True).then_inc(S.mv, 1)
-        g.scalar.wait_ge(S.mu, k + 1)
-        g.scalar.activation(T.yb[:, cols(j)], bu, ActivationFunctionType.Relu).then_inc(S.rl, 1)
-        g.vector.wait_ge(S.rl, k + 1)
-        g.vector.wait_ge(S.mv, k + 1)
-        g.vector.tensor_tensor(T.yb[:, cols(j)], T.yb[:, cols(j)], bv, AluOpType.mult).then_inc(S.yd, 1)
-        if k in stores:
-            js = sorted(T.rank_of(c) for c in stores[k])
-            lo, hi = js[0] * NC, (js[-1] + 1) * NC
-            g.sync.wait_ge(S.yd, k + 1)
-            g.sync.dma_start(T.y[:, lo:hi], T.yb[:, lo:hi]).then_inc(S.st, 16)
+        a, b, n = j * NC + c0, j * NC + c1, c1 - c0
+        bu = T.ps[:, (2 * (m % 4)) * 512:(2 * (m % 4)) * 512 + n]
+        bv = T.ps[:, (2 * (m % 4) + 1) * 512:(2 * (m % 4) + 1) * 512 + n]
+        if q != core:
+            if c0 == 0:
+                g.tensor.wait_ge(S["a%d" % j], need[q][0])
+                g.tensor.wait_ge(S["p%d" % j], need[q][1])
+            if c1 == NC:
+                g.tensor.wait_ge(S["b%d" % j], need[q][2])
+        if m >= 4:
+            g.tensor.wait_ge(S.rl, m - 3)
+            g.tensor.wait_ge(S.yd, m - 3)
+        g.tensor.matmul_mx(bu, T.qu[:], T.su[:], T.qx[:, a:b], T.sx[:, a:b], True, True).then_inc(S.mu, 1)
+        g.tensor.matmul_mx(bv, T.qv[:], T.sv[:], T.qx[:, a:b], T.sx[:, a:b], True, True).then_inc(S.mv, 1)
+        g.scalar.wait_ge(S.mu, m + 1)
+        g.scalar.activation(T.yb[:, a:b], bu, ActivationFunctionType.Relu).then_inc(S.rl, 1)
+        g.vector.wait_ge(S.rl, m + 1)
+        g.vector.wait_ge(S.mv, m + 1)
+        g.vector.tensor_tensor(T.yb[:, a:b], T.yb[:, a:b], bv, AluOpType.mult).then_inc(S.yd, 1)
+        if m == 0:
+            g.sync.wait_ge(S.go1, 1)
+        if m == 2:
+            g.sync.wait_ge(S.go2, 1)
+        if m < len(units) - 1:
+            g.sync.wait_ge(S.yd, m + 1)
+            g.sync.dma_start(T.y[:, a:b], T.yb[:, a:b]).then_inc(S.st, 16)
             nst += 16
+        else:
+            g.scalar.wait_ge(S.yd, m + 1)
+            g.scalar.dma_start(T.y[:, a:b], T.yb[:, a:b]).then_inc(S.st2, 16)
     g.sync.wait_ge(S.st, nst)
+    g.scalar.wait_ge(S.st2, 16)

from concourse.bass import DstId, RemoteDMATransfer
from concourse.mybir import dt, AluOpType, ActivationFunctionType

N = 8
NC = 256
H = NC // 2
WORLD = 256

SCRATCH = {
    "xb": ("sbuf", [128, 4 * NC], "bfloat16"),
    "ub": ("sbuf", [128, 512], "bfloat16"),
    "vb": ("sbuf", [128, 512], "bfloat16"),
    "qx": ("sbuf", [128, N * NC], "float8_e4m3fn_x4"),
    "sx": ("sbuf", [128, N * NC], "uint8"),
    "qu": ("sbuf", [128, 128], "float8_e4m3fn_x4"),
    "su": ("sbuf", [128, 128], "uint8"),
    "qv": ("sbuf", [128, 128], "float8_e4m3fn_x4"),
    "sv": ("sbuf", [128, 128], "uint8"),
    "yb": ("sbuf", [128, N * NC], "float32"),
    "ps": ("psum", [128, 8 * 512], "float32"),
}
SEMAPHORES = (["lxa", "lxb", "lw", "qa", "qb", "qw", "mu", "mv", "rl", "yd", "st", "st2", "sent", "go1", "go2"]
              + ["%s%d" % (p, j) for p in "apb" for j in range(N)])


def _count(mask):
    return bin(mask).count("1")


def _roles(core, T, topo):
    out = {}
    for q in T.cores:
        if q == core:
            continue
        if topo.host(q) == topo.host(core) and topo.chip(q) == topo.chip(core):
            kind = "peer"
        elif topo.mates(core, q):
            kind = "mate"
        elif topo.same_plane(core, q):
            kind = "plane"
        else:
            kind = "far"
        out[(kind, topo.die(q) == topo.die(core))] = q
    return out


def _relay_of(r, T, topo):
    role = _roles(r, T, topo)
    for c in range(WORLD):
        if (c not in T.cores and topo.host(c) == topo.host(r) and topo.chip(c) == topo.chip(r)
                and topo.die(c) == topo.die(r) and topo.may_write(c, role[("mate", True)])
                and topo.may_write(c, role[("mate", False)])):
            return c
    return None


def _piece(T, j, p):
    lo = j * NC
    if p == "a":
        return T.qx[:, lo:lo + H].bitcast(dt.uint8)
    if p == "b":
        return T.qx[:, lo + H:lo + NC].bitcast(dt.uint8)
    return T.sx[:, lo:lo + NC]


def _transfer(T, topo, core, j, p, dests, mask):
    ids = []
    for d in dests:
        rid, pid = topo.addr(d, core)
        ids.append(DstId(rid=rid, pnc=pid))
    return RemoteDMATransfer(dst_ids=ids, dma_engine_mask=mask, remote_sem=T.sem["%s%d" % (p, j)],
                             srcs=[_piece(T, j, p)], dsts=[_piece(T, j, p) for _ in dests])


def _relay_program(g, core, r, T, topo):
    S = T.sem
    role = _roles(r, T, topo)
    j = T.rank_of(r)
    mate, mate2 = role[("mate", True)], role[("mate", False)]
    out = topo.mask(core, mate) & topo.mask(core, mate2)
    off_r = topo.mask(r, mate) & topo.mask(r, role[("far", True)]) & topo.mask(r, role[("plane", True)])
    got = _count(topo.mask(r, core) & ~off_r)
    for p in "apb":
        g.wait_ge(S["%s%d" % (p, j)], got)
        g.remote_dma_fused([_transfer(T, topo, core, j, p, [mate, mate2], out)], local_sem=S.sent)
    g.wait_ge(S.sent, 3 * _count(out))


def rank_program(g, core, T, topo):
    rank = T.rank_of(core)
    if rank is None:
        for r in T.cores:
            if _relay_of(r, T, topo) == core:
                _relay_program(g, core, r, T, topo)
        return
    S = T.sem
    role = _roles(core, T, topo)
    peer = role[("peer", False)]
    far, plane, mate = role[("far", True)], role[("plane", True)], role[("mate", True)]
    far2, plane2, mate2 = role[("far", False)], role[("plane", False)], role[("mate", False)]
    relay = _relay_of(core, T, topo)
    off = topo.mask(core, far) & topo.mask(core, plane) & topo.mask(core, mate)
    every = topo.mask(core, peer) & topo.mask(core, relay)
    stay = every & ~off
    n_off, n_stay, n_every = _count(off), _count(stay), _count(every)
    n_relay = _count(topo.mask(relay, mate) & topo.mask(relay, mate2))
    sent = [0]

    def call(transfers, engines):
        g.remote_dma_fused(transfers, local_sem=S.sent)
        sent[0] += engines

    def tr(j, p, dests, mask):
        return _transfer(T, topo, core, j, p, dests, mask)

    g.sync.dma_start(T.xb[:, 0:4 * H], T.x[:, 0:4 * H]).then_inc(S.lxa, 16)
    g.sync.dma_start(T.xb[:, 4 * H:4 * NC], T.x[:, 4 * H:4 * NC]).then_inc(S.lxb, 16)
    g.sync.dma_start(T.ub[:], T.u[:]).then_inc(S.lw, 16)
    g.sync.dma_start(T.vb[:], T.v[:]).then_inc(S.lw, 16)

    lo = rank * NC
    g.vector.wait_ge(S.lxa, 16)
    g.vector.quantize_mx(T.qx[:, lo:lo + H], T.sx[:, lo:lo + H], T.xb[:, 0:4 * H]).then_inc(S.qa, 1)
    g.vector.wait_ge(S.lxb, 16)
    g.vector.quantize_mx(T.qx[:, lo + H:lo + NC], T.sx[:, lo + H:lo + NC], T.xb[:, 4 * H:4 * NC]).then_inc(S.qb, 1)
    g.vector.wait_ge(S.lw, 32)
    g.vector.quantize_mx(T.qu[:], T.su[:], T.ub[:]).then_inc(S.qw, 1)
    g.vector.quantize_mx(T.qv[:], T.sv[:], T.vb[:]).then_inc(S.qw, 1)

    g.wait_ge(S.qa, 1)
    call([tr(rank, "a", [far, plane], off), tr(rank, "a", [relay, peer], stay)], n_off + n_stay)
    g.wait_ge(S.qb, 1)
    call([tr(rank, "p", [far, plane], off), tr(rank, "p", [relay, peer], stay)], n_off + n_stay)
    call([tr(rank, "b", [far, plane], off), tr(rank, "b", [relay, peer], stay)], n_off + n_stay)
    g.sem_inc(S.go1, 1)
    jf, jp = T.rank_of(far), T.rank_of(plane)
    for p in "ap":
        g.wait_ge(S["%s%d" % (p, jf)], n_off)
        g.wait_ge(S["%s%d" % (p, jp)], n_off)
        call([tr(jf, p, [peer], stay), tr(jp, p, [peer], off)], n_stay + n_off)
    for j in (jf, jp):
        g.wait_ge(S["b%d" % j], n_off)
        call([tr(j, "b", [peer], every)], n_every)
    g.sem_inc(S.go2, 1)
    g.wait_ge(S.sent, sent[0])

    need = {peer: (n_stay, n_stay, n_stay), far: (n_off, n_off, n_off), plane: (n_off, n_off, n_off),
            mate: (n_relay, n_relay, n_relay), mate2: (n_relay, n_relay, n_relay),
            far2: (n_stay, n_stay, n_every), plane2: (n_off, n_off, n_every)}

    units = [(core, 0, NC), (peer, 0, NC), (far, 0, NC), (plane, 0, NC), (far2, 0, H), (plane2, 0, H),
             (mate, 0, NC), (mate2, 0, NC), (far2, H, NC), (plane2, H, NC)]
    g.tensor.wait_ge(S.qw, 2)
    g.tensor.wait_ge(S.qa, 1)
    g.tensor.wait_ge(S.qb, 1)
    nst = 0
    for m, (q, c0, c1) in enumerate(units):
        j = T.rank_of(q)
        a, b, n = j * NC + c0, j * NC + c1, c1 - c0
        bu = T.ps[:, (2 * (m % 4)) * 512:(2 * (m % 4)) * 512 + n]
        bv = T.ps[:, (2 * (m % 4) + 1) * 512:(2 * (m % 4) + 1) * 512 + n]
        if q != core:
            if c0 == 0:
                g.tensor.wait_ge(S["a%d" % j], need[q][0])
                g.tensor.wait_ge(S["p%d" % j], need[q][1])
            if c1 == NC:
                g.tensor.wait_ge(S["b%d" % j], need[q][2])
        if m >= 4:
            g.tensor.wait_ge(S.rl, m - 3)
            g.tensor.wait_ge(S.yd, m - 3)
        g.tensor.matmul_mx(bu, T.qu[:], T.su[:], T.qx[:, a:b], T.sx[:, a:b], True, True).then_inc(S.mu, 1)
        g.tensor.matmul_mx(bv, T.qv[:], T.sv[:], T.qx[:, a:b], T.sx[:, a:b], True, True).then_inc(S.mv, 1)
        g.scalar.wait_ge(S.mu, m + 1)
        g.scalar.activation(T.yb[:, a:b], bu, ActivationFunctionType.Relu).then_inc(S.rl, 1)
        g.vector.wait_ge(S.rl, m + 1)
        g.vector.wait_ge(S.mv, m + 1)
        g.vector.tensor_tensor(T.yb[:, a:b], T.yb[:, a:b], bv, AluOpType.mult).then_inc(S.yd, 1)
        if m == 0:
            g.sync.wait_ge(S.go1, 1)
        if m == 2:
            g.sync.wait_ge(S.go2, 1)
        if m < len(units) - 1:
            g.sync.wait_ge(S.yd, m + 1)
            g.sync.dma_start(T.y[:, a:b], T.yb[:, a:b]).then_inc(S.st, 16)
            nst += 16
        else:
            g.scalar.wait_ge(S.yd, m + 1)
            g.scalar.dma_start(T.y[:, a:b], T.yb[:, a:b]).then_inc(S.st2, 16)
    g.sync.wait_ge(S.st, nst)
    g.scalar.wait_ge(S.st2, 16)
